import numpy as np
import ml_dtypes


def mxq(x, axis, fmt="e4m3"):
    dtype, down = {"e4m3": (ml_dtypes.float8_e4m3fn, 7), "e5m2": (ml_dtypes.float8_e5m2, 14)}[fmt]
    v = np.moveaxis(np.asarray(x, np.float32).astype(ml_dtypes.bfloat16).astype(np.float64), axis, -1)
    blocks = v.reshape(v.shape[:-1] + (-1, 32))
    amax = np.abs(blocks).max(-1, keepdims=True)
    byte = np.maximum(np.where(amax > 0, np.frexp(amax)[1] - 1 + 127, 0) - down, 1)
    scale = np.exp2(byte - 127.0)
    codes = (blocks / scale).astype(np.float32).astype(dtype).astype(np.float64)
    return np.moveaxis((codes * scale).reshape(v.shape), -1, axis)


WIDE = False


def mx_kscale(k):
    if not WIDE:
        return np.ones(k)
    levels = np.array([10, -10, 5, -5, 0])
    if k % 512:
        return np.exp2(np.random.permutation(np.resize(levels, k // 32))).repeat(32)
    a = np.empty((k // 512, 16))
    for p in range(k // 512):
        a[p, :8] = np.random.permutation(np.resize(levels, 8))
        for g in range(8):
            far = levels[np.abs(levels - a[p, g]) >= 10]
            a[p, g + 8] = far[np.random.randint(len(far))]
    return np.exp2(a.ravel()).repeat(32)


def f64(x):
    return np.asarray(x).astype(np.float64)


def striped(idx):
    return np.tile(idx.reshape(-1, 16).T, (8, 1)).astype(np.uint16)


def unstriped(offs):
    return offs[:16].T.reshape(-1).astype(np.int64)


def striped8(idx):
    return np.concatenate([x.reshape(-1, 16).T for x in idx]).astype(np.uint16)


def runs(offs, k):
    lists = np.stack([offs[16 * r : 16 * r + 16].T.reshape(-1) for r in range(8)]).astype(np.int64)
    return lists[np.arange(k) % 512 // 64]


def pack_weight(w):
    k, n = w.shape
    w = f64(np.asarray(w, np.float32).astype(ml_dtypes.bfloat16)).reshape(k // 32, 32, n)
    amax = np.abs(w).max(1)
    byte = np.clip(np.where(amax > 0, np.frexp(amax)[1] - 1 + 127 - 7, 1), 1, 254)
    scaled = (w * np.exp2(127.0 - byte)[:, None, :]).reshape(k, n).astype(np.float32)
    words = np.ascontiguousarray(scaled.reshape(k // 512, 128, 4, n).transpose(0, 1, 3, 2)).astype(ml_dtypes.float8_e4m3fn).view(np.uint8)
    return words, np.ascontiguousarray(byte.astype(np.uint8).reshape(k // 512, 16, n))


def unpack_weight(words, scales):
    g, p, n, _ = words.shape
    vals = np.ascontiguousarray(words).view(ml_dtypes.float8_e4m3fn).astype(np.float64) * np.repeat(np.exp2(scales.astype(np.float64) - 127.0), 8, axis=1)[..., None]
    return vals.transpose(0, 1, 3, 2).reshape(g * 512, n)

def planes(y):
    n, m = y.shape
    v = y.astype(np.float32).astype(ml_dtypes.bfloat16).astype(np.float64).reshape(n // 32, 32, m)
    top = np.abs(v).max(1)
    byte = np.clip(np.where(top > 0, np.frexp(top)[1] - 1 + 127 - 7, 1), 1, 254)
    codes = (v * np.exp2(127.0 - byte)[:, None, :]).reshape(n, m).astype(np.float32).astype(ml_dtypes.float8_e4m3fn).view(np.uint8)
    words = codes.reshape(n // 512, 128, 4, m).transpose(0, 1, 3, 2)
    return np.ascontiguousarray(words), np.ascontiguousarray(byte.astype(np.uint8).reshape(n // 512, 16, m))


K, T, S, G, H, W, U = 512, 1024, 256, 2048, 512, 128, 512


def setup_inputs():
    n = np.random.standard_normal
    s = mx_kscale(K)[:, None]
    packed_xT = pack_weight(n((K, T)) * s)
    packed_dT = pack_weight(n((K, G)) / s)
    perm = np.random.permutation(S)
    perm2 = np.random.permutation(U)
    return {
        "x_words": packed_xT[0],
        "x_scales": packed_xT[1],
        "d_words": packed_dT[0],
        "d_scales": packed_dT[1],
        "gs": (np.random.uniform(0.5, 1.5, (K, 1)) * s).astype(np.float32),
        "offs": striped(np.random.permutation(T)[:S]),
        "ka": striped8(np.random.randint(0, G, (8, H))),
        "kb": striped8(np.random.randint(0, G, (8, H))),
        "n1": striped(perm[:W]),
        "n2": striped(perm[W:]),
        "k1": striped8(np.random.randint(0, G, (8, H))),
        "k2": striped8(np.random.randint(0, G, (8, H))),
        "hz": striped8(np.random.randint(0, T, (8, S))),
        "n3": striped(perm2[:S]),
        "n4": striped(perm2[S:]),
        "n5": striped(np.random.permutation(S)),
        "n6": striped(np.random.permutation(S)),
    }


def reference(x_words, x_scales, d_words, d_scales, gs, offs, ka, kb, n1, n2, k1, k2, hz, n3, n4, n5, n6):
    d_k1 = unpack_weight(d_words, d_scales)[np.arange(K)[:, None], runs(k1, K)]
    d_ka = unpack_weight(d_words, d_scales)[np.arange(K)[:, None], runs(ka, K)]
    xq = unpack_weight(x_words, x_scales)[:, unstriped(offs)]
    d_kb = unpack_weight(d_words, d_scales)[np.arange(K)[:, None], runs(kb, K)]
    h = 0.0625 * (d_ka.T @ xq + d_kb.T @ xq)
    pa = h[:, unstriped(n1)]
    pb = h[:, unstriped(n2)]
    rb = pa - pb
    ra = 0.75 * (pa + pb)
    ua = np.zeros((H, S))
    ua[:, unstriped(n1)] = ra
    ub = ua.copy()
    ub[:, unstriped(n2)] = rb
    z = f64(gs) * ub
    d_k2 = unpack_weight(d_words, d_scales)[np.arange(K)[:, None], runs(k2, K)]
    x_hz = unpack_weight(x_words, x_scales)[np.arange(K)[:, None], runs(hz, K)]
    h2 = 0.0625 * ((d_k1.T @ mxq(z, 0, "e4m3") + d_k2.T @ x_hz))
    st = h2 - h2[:, unstriped(n5)]
    up = np.maximum(st, st[:, unstriped(n6)])
    ph = np.zeros((H, U))
    ph[:, unstriped(n3)] = st
    out = ph.copy()
    out[:, unstriped(n4)] = up
    return (out,) + planes(out)

@@ -1,0 +1,251 @@
+from contextlib import ExitStack
+
+import concourse.mybir as mybir
+
+F32 = mybir.dt.float32
+BF16 = mybir.dt.bfloat16
+I32 = mybir.dt.int32
+U32 = mybir.dt.uint32
+U16 = mybir.dt.uint16
+U8 = mybir.dt.uint8
+FP8X4 = mybir.dt.float8_e4m3fn_x4
+ALU = mybir.AluOpType
+COPY = mybir.ActivationFunctionType.Copy
+
+P = 128
+PACK = 4
+K, T, S, G, H, W, U = 512, 1024, 256, 2048, 512, 128, 512
+SPARE = 16
+ALIGN = 64
+
+FLOPS = 4 * 2 * K * H * S
+
+
+def tile_picked_atzmhhaarpagew_none_po_kernel(
+    tc, x_words, x_scales, d_words, d_scales, gs, offs, ka, kb, n1, n2, k1, k2, hz, n3, n4, n5, n6, out_0, out_1, out_2
+):
+    nc = tc.nc
+    with ExitStack() as ctx:
+        sb = ctx.enter_context(tc.tile_pool(name="sb", bufs=1))
+        ps = ctx.enter_context(tc.psum_pool(name="ps", bufs=1))
+
+        def new(shape, dtype, name, tag=None):
+            return sb.tile(shape, dtype, name=name, tag=tag or name, align_bytes=ALIGN)
+
+        def load_list(src, name):
+            tile = new(list(src.shape), U16, name)
+            nc.sync.dma_start(tile[:], src)
+            return tile
+
+        def load_scales(src, width, name):
+            tile = new([P, width], U8, name)
+            rows = src[0].bitcast(I32).unsqueeze(1).to_broadcast([16, 8, width // 4])
+            nc.sync.dma_start(tile[:].bitcast(I32), rows)
+            return tile
+
+        def load_words(src, width, name):
+            tile = new([P, width], I32, name)
+            nc.sync.dma_start(tile[:], src[0].rearrange("p c r -> p (c r)").bitcast(I32))
+            return tile
+
+        def zeroed_plane(width, name, tag=None):
+            tile = new([P, width], U8, name, tag)
+            nc.vector.memset(tile[:].bitcast(I32), 0)
+            return tile
+
+        def gather_bytes(dst, table, lst):
+            nc.vector.tensor_copy(dst, table[:].indirect(lst[:]))
+
+        def gather_words(dst, table, lst):
+            nc.vector.tensor_copy(dst[:].bitcast(U32), table[:].bitcast(U32).indirect(lst[:]))
+
+        def deal(dst, src):
+            nc.vector.tensor_copy(
+                dst[:].rearrange("p (t m) -> p m t", t=PACK), src[:].rearrange("p (m t) -> p m t", t=PACK)
+            )
+
+        def place_rows(plane, first, src, queue):
+            for j in range(4):
+                queue.dma_start(plane[:].bitcast(I32)[first + j : P : 32, :], src[:].bitcast(I32)[8 * j : P : 32, :])
+
+        def mx(acc, words, plane, first, t, rhs, rhs_plane, start, stop):
+            nc.tensor.matmul_mx(
+                out=acc,
+                lhsT=words[:, t * P : (t + 1) * P].bitcast(FP8X4),
+                lhsT_scale=plane[first:P, t * P : (t + 1) * P],
+                rhs=rhs.bitcast(FP8X4),
+                rhs_scale=rhs_plane,
+                start=start,
+                stop=stop,
+            )
+
+        ka_l = load_list(ka, "ka_l")
+        kb_l = load_list(kb, "kb_l")
+        d_bytes = load_scales(d_scales, G, "d_bytes")
+        offs_l = load_list(offs, "offs_l")
+        x_bytes = load_scales(x_scales, T, "x_bytes")
+        d_tab = load_words(d_words, G, "d_tab")
+        n1_l = load_list(n1, "n1_l")
+        n2_l = load_list(n2, "n2_l")
+        hz_l = load_list(hz, "hz_l")
+        k1_l = load_list(k1, "k1_l")
+        k2_l = load_list(k2, "k2_l")
+        x_tab = load_words(x_words, T, "x_tab")
+
+        ab_rows = zeroed_plane(H, "ab_rows")
+        xq_plane = zeroed_plane(S, "xq_plane")
+        k12_rows = zeroed_plane(H, "k12_rows", "slot_z")
+        hz_plane = zeroed_plane(S, "hz_plane")
+
+        ka_picked = new([P, H], U8, "ka_picked")
+        kb_picked = new([P, H], U8, "kb_picked")
+        xq_picked = new([P, S], U8, "xq_picked")
+        gather_bytes(ka_picked[:], d_bytes, ka_l)
+        place_rows(ab_rows, 0, ka_picked, nc.scalar)
+        gather_bytes(kb_picked[:], d_bytes, kb_l)
+        place_rows(ab_rows, 4, kb_picked, nc.scalar)
+        gather_bytes(xq_picked[:], x_bytes, offs_l)
+        place_rows(xq_plane, 0, xq_picked, nc.sync)
+
+        n5_l = load_list(n5, "n5_l")
+        n6_l = load_list(n6, "n6_l")
+        n3_l = load_list(n3, "n3_l")
+        n4_l = load_list(n4, "n4_l")
+        gs_sb = new([P, PACK], F32, "gs_sb")
+        nc.sync.dma_start(gs_sb[:], gs.rearrange("(p t) o -> p (t o)", t=PACK))
+
+        ka_raw = new([P, H], I32, "ka_raw")
+        kb_raw = new([P, H], I32, "kb_raw", "slot_hzb")
+        ka_w = new([P, H], I32, "ka_w")
+        kb_w = new([P, H], I32, "kb_w")
+        xq_w = new([P, S], I32, "xq_w")
+        ab_plane = new([P, H], U8, "ab_plane")
+        gather_words(ka_raw, d_tab, ka_l)
+        gather_words(kb_raw, d_tab, kb_l)
+        deal(ka_w, ka_raw)
+        gather_words(xq_w, x_tab, offs_l)
+        deal(ab_plane, ab_rows)
+        deal(kb_w, kb_raw)
+
+        h_ps = [ps.tile([P, S], F32, name=f"h_ps{t}") for t in range(PACK)]
+        for t in range(PACK):
+            mx(h_ps[t][:], ka_w, ab_plane, 0, t, xq_w[:], xq_plane[:], True, False)
+            mx(h_ps[t][:], kb_w, ab_plane, 4, t, xq_w[:], xq_plane[:], False, True)
+
+        hz_picked = new([P, S], U8, "hz_picked", "slot_hzb")
+        gather_bytes(hz_picked[:], x_bytes, hz_l)
+        place_rows(hz_plane, 0, hz_picked, nc.sync)
+
+        def leave_psum(dst, acc, t):
+            if t == 0:
+                nc.scalar.activation(dst, acc, COPY, scale=0.0625)
+            else:
+                nc.vector.tensor_scalar(dst, acc, 0.0625, None, ALU.mult)
+
+        h = [new([P, S], F32, f"h{t}", f"slot_h{t}") for t in range(PACK)]
+        pab = [new([P, 2 * W], F32, f"pab{t}", f"slot{t}") for t in range(PACK)]
+        rab = [new([P, 2 * W], F32, f"rab{t}") for t in range(PACK)]
+        ub = [new([P, S], F32, f"ub{t}") for t in range(PACK)]
+        for t in range(PACK):
+            leave_psum(h[t][:], h_ps[t][:], t)
+            nc.scalar.activation(pab[t][:, :W], h[t][:].indirect(n1_l[:]), COPY)
+            nc.scalar.activation(pab[t][:, W:], h[t][:].indirect(n2_l[:]), COPY)
+
+        def pair_sums(t):
+            nc.vector.tensor_tensor(rab[t][:, :W], pab[t][:, :W], pab[t][:, W:], ALU.add)
+            nc.vector.tensor_tensor(rab[t][:, W:], pab[t][:, :W], pab[t][:, W:], ALU.subtract)
+
+        k1_picked = new([P, H], U8, "k1_picked", "slot1")
+        k2_picked = new([P, H], U8, "k2_picked", "slot2")
+        hz_w = new([P, S], I32, "hz_w", "slot0")
+        pair_sums(0)
+        pair_sums(1)
+        gather_words(hz_w, x_tab, hz_l)
+        pair_sums(2)
+        gather_bytes(k1_picked[:], d_bytes, k1_l)
+        place_rows(k12_rows, 0, k1_picked, nc.sync)
+        pair_sums(3)
+        gather_bytes(k2_picked[:], d_bytes, k2_l)
+        place_rows(k12_rows, 4, k2_picked, nc.sync)
+
+        for t in range(PACK + 1):
+            if t < PACK:
+                nc.scalar.activation(ub[t][:].indirect(n1_l[:]), rab[t][:, :W], COPY, scale=0.75)
+            if t > 0:
+                nc.scalar.activation(ub[t - 1][:].indirect(n2_l[:]), rab[t - 1][:, W:], COPY)
+
+        k2_raw = new([P, H], I32, "k2_raw", "slot3")
+        k1_raw = new([P, H], I32, "k1_raw", "slot_h3")
+        k2_w = new([P, H], I32, "k2_w")
+        k1_w = new([P, H], I32, "k1_w")
+        k12_plane = new([P, H], U8, "k12_plane")
+        z16 = new([P, S, PACK], BF16, "z16", "slot_z")
+
+        def round_z(t):
+            nc.vector.tensor_scalar(z16[:, :, t], ub[t][:], gs_sb[:, t : t + 1], None, ALU.mult)
+
+        gather_words(k2_raw, d_tab, k2_l)
+        gather_words(k1_raw, d_tab, k1_l)
+        deal(k2_w, k2_raw)
+        deal(k1_w, k1_raw)
+        deal(k12_plane, k12_rows)
+        for t in range(PACK):
+            round_z(t)
+        z_w = new([P, S], I32, "z_w")
+        z_plane = new([P, S], U8, "z_plane")
+        nc.vector.quantize_mx(out=z_w[:].bitcast(FP8X4), scales=z_plane[:], in_=z16[:].rearrange("p c t -> p (c t)"))
+
+        h2_ps = [ps.tile([P, S], F32, name=f"h2_ps{t}") for t in range(PACK)]
+        for t in range(PACK):
+            mx(h2_ps[t][:], k2_w, k12_plane, 4, t, hz_w[:], hz_plane[:], True, False)
+        for t in range(PACK):
+            mx(h2_ps[t][:], k1_w, k12_plane, 0, t, z_w[:], z_plane[:], False, True)
+
+        h2 = [new([P, S + SPARE], F32, f"h2_{t}") for t in range(PACK)]
+        st = [new([P, S + SPARE], F32, f"st{t}") for t in range(PACK)]
+        h2_at = [new([P, S], F32, f"h2_at{t}") for t in range(PACK)]
+        st_at = [new([P, S], F32, f"st_at{t}") for t in range(PACK)]
+        up = [new([P, S], F32, f"up{t}") for t in range(PACK)]
+        page = [new([P, U], F32, f"page{t}") for t in range(PACK)]
+        page16 = new([P, U, PACK], BF16, "page16")
+        out_rows = out_0.rearrange("(p t) w -> t p w", t=PACK)
+        half = U // 2
+
+        def make_st(t):
+            leave_psum(h2[t][:, :S], h2_ps[t][:], t)
+            nc.scalar.activation(h2_at[t][:], h2[t][:].indirect(n5_l[:]), COPY)
+            nc.vector.tensor_tensor(st[t][:, :S], h2[t][:, :S], h2_at[t][:], ALU.subtract)
+
+        def make_up(t):
+            nc.scalar.activation(st_at[t][:], st[t][:].indirect(n6_l[:]), COPY)
+            nc.vector.tensor_tensor(up[t][:], st[t][:, :S], st_at[t][:], ALU.max)
+            nc.scalar.activation(page[t][:].indirect(n3_l[:]), st[t][:, :S], COPY)
+
+        def finish(t):
+            nc.scalar.activation(page[t][:].indirect(n4_l[:]), up[t][:], COPY)
+            nc.sync.dma_start(out_rows[t], page[t][:])
+            for c in range(2):
+                cols = slice(c * half, (c + 1) * half)
+                nc.vector.tensor_copy(page16[:, cols, t], page[t][:, cols])
+
+        for step in range(PACK + 2):
+            if step < PACK:
+                make_st(step)
+            if 1 <= step <= PACK:
+                make_up(step - 1)
+            if step >= 2:
+                finish(step - 2)
+
+        out_w = new([P, U], I32, "out_w")
+        out_plane = new([P, U], U8, "out_plane")
+        words_out = out_1[0].rearrange("p c r -> p (c r)").bitcast(I32)
+        for c in range(2):
+            cols = slice(c * half, (c + 1) * half)
+            nc.vector.quantize_mx(
+                out=out_w[:, cols].bitcast(FP8X4),
+                scales=out_plane[:, cols],
+                in_=page16[:, cols, :].rearrange("p c t -> p (c t)"),
+            )
+            nc.sync.dma_start(words_out[:, cols], out_w[:, cols])
+        for q in range(4):
+            nc.scalar.dma_start(out_2[0].bitcast(I32)[4 * q : 4 * q + 4, :], out_plane[:].bitcast(I32)[32 * q : 32 * q + 4, :])

@@ -1,6 +1,7 @@
 from contextlib import ExitStack
 
 import concourse.mybir as mybir
+from concourse.masks import make_identity
 
 F32 = mybir.dt.float32
 BF16 = mybir.dt.bfloat16
@@ -66,46 +67,49 @@ def tile_picked_atzmhhaarpagew_none_po_kernel(
 
         def place_rows(plane, first, src, queue):
             for j in range(4):
-                queue.dma_start(plane[:].bitcast(I32)[first + j : P : 32, :], src[:].bitcast(I32)[8 * j : P : 32, :])
+                queue.dma_start(plane[:].bitcast(I32)[first + j : P : 32, :], src.bitcast(I32)[8 * j : P : 32, :])
 
-        def mx(acc, words, plane, first, t, rhs, rhs_plane, start, stop):
+        def mx(acc, lhs, lhs_plane, rhs, rhs_plane, start, stop):
             nc.tensor.matmul_mx(
                 out=acc,
-                lhsT=words[:, t * P : (t + 1) * P].bitcast(FP8X4),
-                lhsT_scale=plane[first:P, t * P : (t + 1) * P],
+                lhsT=lhs.bitcast(FP8X4),
+                lhsT_scale=lhs_plane,
                 rhs=rhs.bitcast(FP8X4),
                 rhs_scale=rhs_plane,
                 start=start,
                 stop=stop,
             )
 
+        def block(n, width=P):
+            return slice(n * width, (n + 1) * width)
+
+        x_bytes = load_scales(x_scales, T, "x_bytes")
+        offs_l = load_list(offs, "offs_l")
+        d_bytes = load_scales(d_scales, G, "d_bytes")
         ka_l = load_list(ka, "ka_l")
         kb_l = load_list(kb, "kb_l")
-        d_bytes = load_scales(d_scales, G, "d_bytes")
-        offs_l = load_list(offs, "offs_l")
-        x_bytes = load_scales(x_scales, T, "x_bytes")
+        x_tab = load_words(x_words, T, "x_tab")
         d_tab = load_words(d_words, G, "d_tab")
         n1_l = load_list(n1, "n1_l")
         n2_l = load_list(n2, "n2_l")
         hz_l = load_list(hz, "hz_l")
         k1_l = load_list(k1, "k1_l")
         k2_l = load_list(k2, "k2_l")
-        x_tab = load_words(x_words, T, "x_tab")
 
-        ab_rows = zeroed_plane(H, "ab_rows")
-        xq_plane = zeroed_plane(S, "xq_plane")
+        xa_plane = zeroed_plane(S + H, "xa_plane")
+        kb_plane = zeroed_plane(H, "kb_plane")
         k12_rows = zeroed_plane(H, "k12_rows", "slot_z")
         hz_plane = zeroed_plane(S, "hz_plane")
+        ident = new([P, P], F32, "ident")
+        make_identity(nc, ident[:])
 
-        ka_picked = new([P, H], U8, "ka_picked")
+        xa_picked = new([P, S + H], U8, "xa_picked")
         kb_picked = new([P, H], U8, "kb_picked")
-        xq_picked = new([P, S], U8, "xq_picked")
-        gather_bytes(ka_picked[:], d_bytes, ka_l)
-        place_rows(ab_rows, 0, ka_picked, nc.scalar)
+        gather_bytes(xa_picked[:, :S], x_bytes, offs_l)
+        gather_bytes(xa_picked[:, S:], d_bytes, ka_l)
+        place_rows(xa_plane, 0, xa_picked[:], nc.scalar)
         gather_bytes(kb_picked[:], d_bytes, kb_l)
-        place_rows(ab_rows, 4, kb_picked, nc.scalar)
-        gather_bytes(xq_picked[:], x_bytes, offs_l)
-        place_rows(xq_plane, 0, xq_picked, nc.sync)
+        place_rows(kb_plane, 0, kb_picked[:], nc.sync)
 
         n5_l = load_list(n5, "n5_l")
         n6_l = load_list(n6, "n6_l")
@@ -114,40 +118,54 @@ def tile_picked_atzmhhaarpagew_none_po_kernel(
         gs_sb = new([P, PACK], F32, "gs_sb")
         nc.sync.dma_start(gs_sb[:], gs.rearrange("(p t) o -> p (t o)", t=PACK))
 
-        ka_raw = new([P, H], I32, "ka_raw")
-        kb_raw = new([P, H], I32, "kb_raw", "slot_hzb")
-        ka_w = new([P, H], I32, "ka_w")
+        xq_w = new([P, S], I32, "xq_w", "slot_hzw")
+        ka_w = new([P, H], I32, "ka_w", "slot_hzb")
         kb_w = new([P, H], I32, "kb_w")
-        xq_w = new([P, S], I32, "xq_w")
-        ab_plane = new([P, H], U8, "ab_plane")
-        gather_words(ka_raw, d_tab, ka_l)
-        gather_words(kb_raw, d_tab, kb_l)
-        deal(ka_w, ka_raw)
         gather_words(xq_w, x_tab, offs_l)
-        deal(ab_plane, ab_rows)
-        deal(kb_w, kb_raw)
+        gather_words(ka_w, d_tab, ka_l)
+        for c in range(2):
+            nc.vector.tensor_copy(
+                kb_w[:, block(c, S)].bitcast(U32), d_tab[:].bitcast(U32).indirect(kb_l[:, block(c, S // 16)])
+            )
 
+        ht_ps = [[ps.tile([P, S], F32, name=f"ht_ps{c}{u}", tag=f"bank{2 * c + u}") for u in range(2)] for c in range(2)]
+        ht = [new([P, PACK, P], F32, f"ht{u}") for u in range(2)]
+        for c in range(2):
+            for u in range(2):
+                mx(ht_ps[c][u][:], xq_w[:, block(u)], xa_plane[:, block(u)],
+                   ka_w[:, block(c, S)], xa_plane[:, block(c + 1, S)], True, False)
+        for c in range(2):
+            for u in range(2):
+                mx(ht_ps[c][u][:], xq_w[:, block(u)], xa_plane[:, block(u)],
+                   kb_w[:, block(c, S)], kb_plane[:, block(c, S)], False, True)
+                nc.scalar.activation(
+                    ht[u][:, :, block(c, P // 2)], ht_ps[c][u][:].rearrange("p (m t) -> p t m", t=PACK), COPY, scale=0.0625
+                )
         h_ps = [ps.tile([P, S], F32, name=f"h_ps{t}") for t in range(PACK)]
         for t in range(PACK):
-            mx(h_ps[t][:], ka_w, ab_plane, 0, t, xq_w[:], xq_plane[:], True, False)
-            mx(h_ps[t][:], kb_w, ab_plane, 4, t, xq_w[:], xq_plane[:], False, True)
+            for u in range(2):
+                nc.tensor.transpose(h_ps[t][:, block(u)], ht[u][:, t, :], ident[:])
 
-        hz_picked = new([P, S], U8, "hz_picked", "slot_hzb")
-        gather_bytes(hz_picked[:], x_bytes, hz_l)
-        place_rows(hz_plane, 0, hz_picked, nc.sync)
+        hk_picked = new([P, S + H], U8, "hk_picked", "slot_hzb")
+        hz_w = new([P, S], I32, "hz_w", "slot_hzw")
+        gather_bytes(hk_picked[:, :S], x_bytes, hz_l)
+        place_rows(hz_plane, 0, hk_picked[:, :S], nc.sync)
+        gather_bytes(hk_picked[:, S:], d_bytes, k1_l)
+        place_rows(k12_rows, 0, hk_picked[:, S:], nc.sync)
+        gather_words(hz_w, x_tab, hz_l)
 
-        def leave_psum(dst, acc, t):
+        def leave_psum(dst, acc, scale, t):
             if t == 0:
-                nc.scalar.activation(dst, acc, COPY, scale=0.0625)
+                nc.scalar.activation(dst, acc, COPY, scale=scale)
             else:
-                nc.vector.tensor_scalar(dst, acc, 0.0625, None, ALU.mult)
+                nc.vector.tensor_scalar(dst, acc, scale, None, ALU.mult)
 
         h = [new([P, S], F32, f"h{t}", f"slot_h{t}") for t in range(PACK)]
         pab = [new([P, 2 * W], F32, f"pab{t}", f"slot{t}") for t in range(PACK)]
         rab = [new([P, 2 * W], F32, f"rab{t}") for t in range(PACK)]
         ub = [new([P, S], F32, f"ub{t}") for t in range(PACK)]
         for t in range(PACK):
-            leave_psum(h[t][:], h_ps[t][:], t)
+            leave_psum(h[t][:], h_ps[t][:], 1.0, t)
             nc.scalar.activation(pab[t][:, :W], h[t][:].indirect(n1_l[:]), COPY)
             nc.scalar.activation(pab[t][:, W:], h[t][:].indirect(n2_l[:]), COPY)
 
@@ -155,18 +173,13 @@ def tile_picked_atzmhhaarpagew_none_po_kernel(
             nc.vector.tensor_tensor(rab[t][:, :W], pab[t][:, :W], pab[t][:, W:], ALU.add)
             nc.vector.tensor_tensor(rab[t][:, W:], pab[t][:, :W], pab[t][:, W:], ALU.subtract)
 
-        k1_picked = new([P, H], U8, "k1_picked", "slot1")
-        k2_picked = new([P, H], U8, "k2_picked", "slot2")
-        hz_w = new([P, S], I32, "hz_w", "slot0")
+        k2_picked = new([P, H], U8, "k2_picked", "slot1")
         pair_sums(0)
         pair_sums(1)
-        gather_words(hz_w, x_tab, hz_l)
-        pair_sums(2)
-        gather_bytes(k1_picked[:], d_bytes, k1_l)
-        place_rows(k12_rows, 0, k1_picked, nc.sync)
-        pair_sums(3)
         gather_bytes(k2_picked[:], d_bytes, k2_l)
-        place_rows(k12_rows, 4, k2_picked, nc.sync)
+        place_rows(k12_rows, 4, k2_picked[:], nc.sync)
+        pair_sums(2)
+        pair_sums(3)
 
         for t in range(PACK + 1):
             if t < PACK:
@@ -181,25 +194,35 @@ def tile_picked_atzmhhaarpagew_none_po_kernel(
         k12_plane = new([P, H], U8, "k12_plane")
         z16 = new([P, S, PACK], BF16, "z16", "slot_z")
 
-        def round_z(t):
-            nc.vector.tensor_scalar(z16[:, :, t], ub[t][:], gs_sb[:, t : t + 1], None, ALU.mult)
+        def round_z(t, cols):
+            nc.vector.tensor_scalar(z16[:, cols, t], ub[t][:, cols], gs_sb[:, t : t + 1], None, ALU.mult)
 
         gather_words(k2_raw, d_tab, k2_l)
         gather_words(k1_raw, d_tab, k1_l)
         deal(k2_w, k2_raw)
         deal(k1_w, k1_raw)
         deal(k12_plane, k12_rows)
-        for t in range(PACK):
-            round_z(t)
+        for t in range(PACK - 1):
+            round_z(t, slice(0, S))
         z_w = new([P, S], I32, "z_w")
         z_plane = new([P, S], U8, "z_plane")
-        nc.vector.quantize_mx(out=z_w[:].bitcast(FP8X4), scales=z_plane[:], in_=z16[:].rearrange("p c t -> p (c t)"))
+        for u in range(2):
+            round_z(PACK - 1, block(u))
+        for u in range(2):
+            nc.vector.quantize_mx(
+                out=z_w[:, block(u)].bitcast(FP8X4),
+                scales=z_plane[:, block(u)],
+                in_=z16[:, block(u), :].rearrange("p c t -> p (c t)"),
+            )
 
-        h2_ps = [ps.tile([P, S], F32, name=f"h2_ps{t}") for t in range(PACK)]
+        h2_ps = [ps.tile([P, S], F32, name=f"h2_ps{t}", tag=f"bank{t}") for t in range(PACK)]
         for t in range(PACK):
-            mx(h2_ps[t][:], k2_w, k12_plane, 4, t, hz_w[:], hz_plane[:], True, False)
-        for t in range(PACK):
-            mx(h2_ps[t][:], k1_w, k12_plane, 0, t, z_w[:], z_plane[:], False, True)
+            mx(h2_ps[t][:], k2_w[:, block(t)], k12_plane[4:P, block(t)], hz_w[:], hz_plane[:], True, False)
+        for u in range(2):
+            mx(h2_ps[0][:, block(u)], k1_w[:, block(0)], k12_plane[:, block(0)],
+               z_w[:, block(u)], z_plane[:, block(u)], False, u == 1)
+        for t in range(1, PACK):
+            mx(h2_ps[t][:], k1_w[:, block(t)], k12_plane[:, block(t)], z_w[:], z_plane[:], False, True)
 
         h2 = [new([P, S + SPARE], F32, f"h2_{t}") for t in range(PACK)]
         st = [new([P, S + SPARE], F32, f"st{t}") for t in range(PACK)]
@@ -212,7 +235,7 @@ def tile_picked_atzmhhaarpagew_none_po_kernel(
         half = U // 2
 
         def make_st(t):
-            leave_psum(h2[t][:, :S], h2_ps[t][:], t)
+            leave_psum(h2[t][:, :S], h2_ps[t][:], 0.0625, t)
             nc.scalar.activation(h2_at[t][:], h2[t][:].indirect(n5_l[:]), COPY)
             nc.vector.tensor_tensor(st[t][:, :S], h2[t][:, :S], h2_at[t][:], ALU.subtract)
 
@@ -224,9 +247,11 @@ def tile_picked_atzmhhaarpagew_none_po_kernel(
         def finish(t):
             nc.scalar.activation(page[t][:].indirect(n4_l[:]), up[t][:], COPY)
             nc.sync.dma_start(out_rows[t], page[t][:])
-            for c in range(2):
-                cols = slice(c * half, (c + 1) * half)
-                nc.vector.tensor_copy(page16[:, cols, t], page[t][:, cols])
+            if t < PACK - 1:
+                nc.vector.tensor_copy(page16[:, :, t], page[t][:])
+            else:
+                nc.vector.tensor_copy(page16[:, :half, t], page[t][:, :half])
+                nc.vector.tensor_copy(page16[:, half:, t], page[t][:, half:])
 
         for step in range(PACK + 2):
             if step < PACK:
@@ -248,4 +273,5 @@ def tile_picked_atzmhhaarpagew_none_po_kernel(
             )
             nc.sync.dma_start(words_out[:, cols], out_w[:, cols])
         for q in range(4):
-            nc.scalar.dma_start(out_2[0].bitcast(I32)[4 * q : 4 * q + 4, :], out_plane[:].bitcast(I32)[32 * q : 32 * q + 4, :])
+            queue = nc.scalar if q % 2 else nc.sync
+            queue.dma_start(out_2[0].bitcast(I32)[4 * q : 4 * q + 4, :], out_plane[:].bitcast(I32)[32 * q : 32 * q + 4, :])

@@ -17,6 +17,8 @@ P = 128
 PACK = 4
 K, T, S, G, H, W, U = 512, 1024, 256, 2048, 512, 128, 512
 SPARE = 16
+PAGE_ORDER = (0, 2, 1, 3)
+SCALAR_COLS = 192
 ALIGN = 64
 
 FLOPS = 4 * 2 * K * H * S
@@ -141,31 +143,32 @@ def tile_picked_atzmhhaarpagew_none_po_kernel(
                 nc.scalar.activation(
                     ht[u][:, :, block(c, P // 2)], ht_ps[c][u][:].rearrange("p (m t) -> p t m", t=PACK), COPY, scale=0.0625
                 )
-        h_ps = [ps.tile([P, S], F32, name=f"h_ps{t}") for t in range(PACK)]
-        for t in range(PACK):
+        h0_ps = [ps.tile([P, P], F32, name=f"h0_ps{u}", tag=f"bank{4 - 4 * u}") for u in range(2)]
+        h_ps = [None] + [ps.tile([P, S], F32, name=f"h_ps{t}", tag=f"bank{4 + t}") for t in range(1, PACK)]
+        for u in range(2):
+            nc.tensor.transpose(h0_ps[u][:], ht[u][:, 0, :], ident[:])
+        for t in range(1, PACK):
             for u in range(2):
                 nc.tensor.transpose(h_ps[t][:, block(u)], ht[u][:, t, :], ident[:])
 
         hk_picked = new([P, S + H], U8, "hk_picked", "slot_hzb")
-        hz_w = new([P, S], I32, "hz_w", "slot_hzw")
         gather_bytes(hk_picked[:, :S], x_bytes, hz_l)
         place_rows(hz_plane, 0, hk_picked[:, :S], nc.sync)
         gather_bytes(hk_picked[:, S:], d_bytes, k1_l)
         place_rows(k12_rows, 0, hk_picked[:, S:], nc.sync)
+        hz_w = new([P, S], I32, "hz_w", "slot_hzw")
         gather_words(hz_w, x_tab, hz_l)
-
-        def leave_psum(dst, acc, scale, t):
-            if t == 0:
-                nc.scalar.activation(dst, acc, COPY, scale=scale)
-            else:
-                nc.vector.tensor_scalar(dst, acc, scale, None, ALU.mult)
 
         h = [new([P, S], F32, f"h{t}", f"slot_h{t}") for t in range(PACK)]
         pab = [new([P, 2 * W], F32, f"pab{t}", f"slot{t}") for t in range(PACK)]
         rab = [new([P, 2 * W], F32, f"rab{t}") for t in range(PACK)]
         ub = [new([P, S], F32, f"ub{t}") for t in range(PACK)]
         for t in range(PACK):
-            leave_psum(h[t][:], h_ps[t][:], 1.0, t)
+            if t == 0:
+                for u in range(2):
+                    nc.scalar.activation(h[t][:, block(u)], h0_ps[u][:], COPY)
+            else:
+                nc.vector.tensor_copy(h[t][:], h_ps[t][:])
             nc.scalar.activation(pab[t][:, :W], h[t][:].indirect(n1_l[:]), COPY)
             nc.scalar.activation(pab[t][:, W:], h[t][:].indirect(n2_l[:]), COPY)
 
@@ -215,13 +218,17 @@ def tile_picked_atzmhhaarpagew_none_po_kernel(
                 in_=z16[:, block(u), :].rearrange("p c t -> p (c t)"),
             )
 
-        h2_ps = [ps.tile([P, S], F32, name=f"h2_ps{t}", tag=f"bank{t}") for t in range(PACK)]
-        for t in range(PACK):
+        h20_ps = [ps.tile([P, P], F32, name=f"h20_ps{u}", tag=f"bank{4 * u}") for u in range(2)]
+        h2_ps = [None] + [ps.tile([P, S], F32, name=f"h2_ps{t}", tag=f"bank{t}") for t in range(1, PACK)]
+        for u in range(2):
+            mx(h20_ps[u][:], k2_w[:, block(0)], k12_plane[4:P, block(0)],
+               hz_w[:, block(u)], hz_plane[:, block(u)], True, False)
+        for t in PAGE_ORDER[1:]:
             mx(h2_ps[t][:], k2_w[:, block(t)], k12_plane[4:P, block(t)], hz_w[:], hz_plane[:], True, False)
         for u in range(2):
-            mx(h2_ps[0][:, block(u)], k1_w[:, block(0)], k12_plane[:, block(0)],
-               z_w[:, block(u)], z_plane[:, block(u)], False, u == 1)
-        for t in range(1, PACK):
+            mx(h20_ps[u][:], k1_w[:, block(0)], k12_plane[:, block(0)],
+               z_w[:, block(u)], z_plane[:, block(u)], False, True)
+        for t in PAGE_ORDER[1:]:
             mx(h2_ps[t][:], k1_w[:, block(t)], k12_plane[:, block(t)], z_w[:], z_plane[:], False, True)
 
         h2 = [new([P, S + SPARE], F32, f"h2_{t}") for t in range(PACK)]
@@ -235,7 +242,11 @@ def tile_picked_atzmhhaarpagew_none_po_kernel(
         half = U // 2
 
         def make_st(t):
-            leave_psum(h2[t][:, :S], h2_ps[t][:], 0.0625, t)
+            if t == 0:
+                nc.scalar.activation(h2[t][:, block(0)], h20_ps[0][:], COPY, scale=0.0625)
+                nc.vector.tensor_scalar(h2[t][:, block(1)], h20_ps[1][:], 0.0625, None, ALU.mult)
+            else:
+                nc.vector.tensor_scalar(h2[t][:, :S], h2_ps[t][:], 0.0625, None, ALU.mult)
             nc.scalar.activation(h2_at[t][:], h2[t][:].indirect(n5_l[:]), COPY)
             nc.vector.tensor_tensor(st[t][:, :S], h2[t][:, :S], h2_at[t][:], ALU.subtract)
 
@@ -251,15 +262,16 @@ def tile_picked_atzmhhaarpagew_none_po_kernel(
                 nc.vector.tensor_copy(page16[:, :, t], page[t][:])
             else:
                 nc.vector.tensor_copy(page16[:, :half, t], page[t][:, :half])
-                nc.vector.tensor_copy(page16[:, half:, t], page[t][:, half:])
+                nc.scalar.activation(page16[:, U - SCALAR_COLS :, t], page[t][:, U - SCALAR_COLS :], COPY)
+                nc.vector.tensor_copy(page16[:, half : U - SCALAR_COLS, t], page[t][:, half : U - SCALAR_COLS])
 
         for step in range(PACK + 2):
             if step < PACK:
-                make_st(step)
+                make_st(PAGE_ORDER[step])
             if 1 <= step <= PACK:
-                make_up(step - 1)
+                make_up(PAGE_ORDER[step - 1])
             if step >= 2:
-                finish(step - 2)
+                finish(PAGE_ORDER[step - 2])
 
         out_w = new([P, U], I32, "out_w")
         out_plane = new([P, U], U8, "out_plane")

@@ -64,12 +64,12 @@ def tile_picked_atzmhhaarpagew_none_po_kernel(
 
         def deal(dst, src):
             nc.vector.tensor_copy(
-                dst[:].rearrange("p (t m) -> p m t", t=PACK), src[:].rearrange("p (m t) -> p m t", t=PACK)
+                dst[:].rearrange("p (t m) -> p m t", t=PACK), src.rearrange("p (m t) -> p m t", t=PACK)
             )
 
         def place_rows(plane, first, src, queue):
             for j in range(4):
-                queue.dma_start(plane[:].bitcast(I32)[first + j : P : 32, :], src.bitcast(I32)[8 * j : P : 32, :])
+                queue.dma_start(plane.bitcast(I32)[first + j : P : 32, :], src.bitcast(I32)[8 * j : P : 32, :])
 
         def mx(acc, lhs, lhs_plane, rhs, rhs_plane, start, stop):
             nc.tensor.matmul_mx(
@@ -109,9 +109,9 @@ def tile_picked_atzmhhaarpagew_none_po_kernel(
         kb_picked = new([P, H], U8, "kb_picked")
         gather_bytes(xa_picked[:, :S], x_bytes, offs_l)
         gather_bytes(xa_picked[:, S:], d_bytes, ka_l)
-        place_rows(xa_plane, 0, xa_picked[:], nc.scalar)
+        place_rows(xa_plane[:], 0, xa_picked[:], nc.scalar)
         gather_bytes(kb_picked[:], d_bytes, kb_l)
-        place_rows(kb_plane, 0, kb_picked[:], nc.sync)
+        place_rows(kb_plane[:], 0, kb_picked[:], nc.sync)
 
         n5_l = load_list(n5, "n5_l")
         n6_l = load_list(n6, "n6_l")
@@ -120,7 +120,7 @@ def tile_picked_atzmhhaarpagew_none_po_kernel(
         gs_sb = new([P, PACK], F32, "gs_sb")
         nc.sync.dma_start(gs_sb[:], gs.rearrange("(p t) o -> p (t o)", t=PACK))
 
-        xq_w = new([P, S], I32, "xq_w", "slot_hzw")
+        xq_w = new([P, S], I32, "xq_w")
         ka_w = new([P, H], I32, "ka_w", "slot_hzb")
         kb_w = new([P, H], I32, "kb_w")
         gather_words(xq_w, x_tab, offs_l)
@@ -151,15 +151,15 @@ def tile_picked_atzmhhaarpagew_none_po_kernel(
             for u in range(2):
                 nc.tensor.transpose(h_ps[t][:, block(u)], ht[u][:, t, :], ident[:])
 
-        hk_picked = new([P, S + H], U8, "hk_picked", "slot_hzb")
-        gather_bytes(hk_picked[:, :S], x_bytes, hz_l)
-        place_rows(hz_plane, 0, hk_picked[:, :S], nc.sync)
-        gather_bytes(hk_picked[:, S:], d_bytes, k1_l)
-        place_rows(k12_rows, 0, hk_picked[:, S:], nc.sync)
-        hz_w = new([P, S], I32, "hz_w", "slot_hzw")
-        gather_words(hz_w, x_tab, hz_l)
+        hk_picked = new([P, 2 * H + S], U8, "hk_picked", "slot_hzb")
+        gather_bytes(hk_picked[:, 2 * H :], x_bytes, hz_l)
+        gather_bytes(hk_picked[:, block(1, H)], d_bytes, k1_l)
+        gather_bytes(hk_picked[:, block(0, H)], d_bytes, k2_l)
+        place_rows(k12_rows[:], 0, hk_picked[:, block(1, H)], nc.sync)
+        place_rows(k12_rows[:], 4, hk_picked[:, block(0, H)], nc.sync)
+        place_rows(hz_plane[:], 0, hk_picked[:, 2 * H :], nc.sync)
 
-        h = [new([P, S], F32, f"h{t}", f"slot_h{t}") for t in range(PACK)]
+        h = [new([P, S], F32, f"h{t}") for t in range(PACK)]
         pab = [new([P, 2 * W], F32, f"pab{t}", f"slot{t}") for t in range(PACK)]
         rab = [new([P, 2 * W], F32, f"rab{t}") for t in range(PACK)]
         ub = [new([P, S], F32, f"ub{t}") for t in range(PACK)]
@@ -176,11 +176,10 @@ def tile_picked_atzmhhaarpagew_none_po_kernel(
             nc.vector.tensor_tensor(rab[t][:, :W], pab[t][:, :W], pab[t][:, W:], ALU.add)
             nc.vector.tensor_tensor(rab[t][:, W:], pab[t][:, :W], pab[t][:, W:], ALU.subtract)
 
-        k2_picked = new([P, H], U8, "k2_picked", "slot1")
+        hz_w = new([P, S], I32, "hz_w", "slot0")
         pair_sums(0)
         pair_sums(1)
-        gather_bytes(k2_picked[:], d_bytes, k2_l)
-        place_rows(k12_rows, 4, k2_picked[:], nc.sync)
+        gather_words(hz_w, x_tab, hz_l)
         pair_sums(2)
         pair_sums(3)
 
@@ -191,7 +190,7 @@ def tile_picked_atzmhhaarpagew_none_po_kernel(
                 nc.scalar.activation(ub[t - 1][:].indirect(n2_l[:]), rab[t - 1][:, W:], COPY)
 
         k2_raw = new([P, H], I32, "k2_raw", "slot3")
-        k1_raw = new([P, H], I32, "k1_raw", "slot_h3")
+        k1_raw = new([P, H], I32, "k1_raw", "slot_z")
         k2_w = new([P, H], I32, "k2_w")
         k1_w = new([P, H], I32, "k1_w")
         k12_plane = new([P, H], U8, "k12_plane")
@@ -201,10 +200,10 @@ def tile_picked_atzmhhaarpagew_none_po_kernel(
             nc.vector.tensor_scalar(z16[:, cols, t], ub[t][:, cols], gs_sb[:, t : t + 1], None, ALU.mult)
 
         gather_words(k2_raw, d_tab, k2_l)
+        deal(k12_plane, k12_rows[:])
+        deal(k2_w, k2_raw[:])
         gather_words(k1_raw, d_tab, k1_l)
-        deal(k2_w, k2_raw)
-        deal(k1_w, k1_raw)
-        deal(k12_plane, k12_rows)
+        deal(k1_w, k1_raw[:])
         for t in range(PACK - 1):
             round_z(t, slice(0, S))
         z_w = new([P, S], I32, "z_w")

@@ -92,11 +92,6 @@ def tile_picked_atzmhhaarpagew_none_po_kernel(
         kb_l = load_list(kb, "kb_l")
         x_tab = load_words(x_words, T, "x_tab")
         d_tab = load_words(d_words, G, "d_tab")
-        n1_l = load_list(n1, "n1_l")
-        n2_l = load_list(n2, "n2_l")
-        hz_l = load_list(hz, "hz_l")
-        k1_l = load_list(k1, "k1_l")
-        k2_l = load_list(k2, "k2_l")
 
         xa_plane = zeroed_plane(S + H, "xa_plane")
         kb_plane = zeroed_plane(H, "kb_plane")
@@ -111,8 +106,13 @@ def tile_picked_atzmhhaarpagew_none_po_kernel(
         gather_bytes(xa_picked[:, S:], d_bytes, ka_l)
         place_rows(xa_plane[:], 0, xa_picked[:], nc.scalar)
         gather_bytes(kb_picked[:], d_bytes, kb_l)
-        place_rows(kb_plane[:], 0, kb_picked[:], nc.sync)
+        place_rows(kb_plane[:], 0, kb_picked[:], nc.scalar)
 
+        hz_l = load_list(hz, "hz_l")
+        k1_l = load_list(k1, "k1_l")
+        k2_l = load_list(k2, "k2_l")
+        n1_l = load_list(n1, "n1_l")
+        n2_l = load_list(n2, "n2_l")
         n5_l = load_list(n5, "n5_l")
         n6_l = load_list(n6, "n6_l")
         n3_l = load_list(n3, "n3_l")

from contextlib import ExitStack

import concourse.mybir as mybir
from concourse.masks import make_identity

F32 = mybir.dt.float32
BF16 = mybir.dt.bfloat16
I32 = mybir.dt.int32
U32 = mybir.dt.uint32
U16 = mybir.dt.uint16
U8 = mybir.dt.uint8
FP8X4 = mybir.dt.float8_e4m3fn_x4
ALU = mybir.AluOpType
COPY = mybir.ActivationFunctionType.Copy

P = 128
PACK = 4
K, T, S, G, H, W, U = 512, 1024, 256, 2048, 512, 128, 512
SPARE = 16
PAGE_ORDER = (0, 2, 1, 3)
SCALAR_COLS = 192
ALIGN = 64

FLOPS = 4 * 2 * K * H * S


def tile_picked_atzmhhaarpagew_none_po_kernel(
    tc, x_words, x_scales, d_words, d_scales, gs, offs, ka, kb, n1, n2, k1, k2, hz, n3, n4, n5, n6, out_0, out_1, out_2
):
    nc = tc.nc
    with ExitStack() as ctx:
        sb = ctx.enter_context(tc.tile_pool(name="sb", bufs=1))
        ps = ctx.enter_context(tc.psum_pool(name="ps", bufs=1))

        def new(shape, dtype, name, tag=None):
            return sb.tile(shape, dtype, name=name, tag=tag or name, align_bytes=ALIGN)

        def load_list(src, name):
            tile = new(list(src.shape), U16, name)
            nc.sync.dma_start(tile[:], src)
            return tile

        def load_scales(src, width, name):
            tile = new([P, width], U8, name)
            rows = src[0].bitcast(I32).unsqueeze(1).to_broadcast([16, 8, width // 4])
            nc.sync.dma_start(tile[:].bitcast(I32), rows)
            return tile

        def load_words(src, width, name):
            tile = new([P, width], I32, name)
            nc.sync.dma_start(tile[:], src[0].rearrange("p c r -> p (c r)").bitcast(I32))
            return tile

        def zeroed_plane(width, name, tag=None):
            tile = new([P, width], U8, name, tag)
            nc.vector.memset(tile[:].bitcast(I32), 0)
            return tile

        def gather_bytes(dst, table, lst):
            nc.vector.tensor_copy(dst, table[:].indirect(lst[:]))

        def gather_words(dst, table, lst):
            nc.vector.tensor_copy(dst[:].bitcast(U32), table[:].bitcast(U32).indirect(lst[:]))

        def deal(dst, src):
            nc.vector.tensor_copy(
                dst[:].rearrange("p (t m) -> p m t", t=PACK), src.rearrange("p (m t) -> p m t", t=PACK)
            )

        def place_rows(plane, first, src, queue):
            for j in range(4):
                queue.dma_start(plane.bitcast(I32)[first + j : P : 32, :], src.bitcast(I32)[8 * j : P : 32, :])

        def mx(acc, lhs, lhs_plane, rhs, rhs_plane, start, stop):
            nc.tensor.matmul_mx(
                out=acc,
                lhsT=lhs.bitcast(FP8X4),
                lhsT_scale=lhs_plane,
                rhs=rhs.bitcast(FP8X4),
                rhs_scale=rhs_plane,
                start=start,
                stop=stop,
            )

        def block(n, width=P):
            return slice(n * width, (n + 1) * width)

        x_bytes = load_scales(x_scales, T, "x_bytes")
        offs_l = load_list(offs, "offs_l")
        d_bytes = load_scales(d_scales, G, "d_bytes")
        ka_l = load_list(ka, "ka_l")
        kb_l = load_list(kb, "kb_l")
        x_tab = load_words(x_words, T, "x_tab")
        d_tab = load_words(d_words, G, "d_tab")

        xa_plane = zeroed_plane(S + H, "xa_plane")
        kb_plane = zeroed_plane(H, "kb_plane")
        k12_rows = zeroed_plane(H, "k12_rows", "slot_z")
        hz_plane = zeroed_plane(S, "hz_plane")
        ident = new([P, P], F32, "ident")
        make_identity(nc, ident[:])

        xa_picked = new([P, S + H], U8, "xa_picked")
        kb_picked = new([P, H], U8, "kb_picked")
        gather_bytes(xa_picked[:, :S], x_bytes, offs_l)
        gather_bytes(xa_picked[:, S:], d_bytes, ka_l)
        place_rows(xa_plane[:], 0, xa_picked[:], nc.scalar)
        gather_bytes(kb_picked[:], d_bytes, kb_l)
        place_rows(kb_plane[:], 0, kb_picked[:], nc.scalar)

        hz_l = load_list(hz, "hz_l")
        k1_l = load_list(k1, "k1_l")
        k2_l = load_list(k2, "k2_l")
        n1_l = load_list(n1, "n1_l")
        n2_l = load_list(n2, "n2_l")
        n5_l = load_list(n5, "n5_l")
        n6_l = load_list(n6, "n6_l")
        n3_l = load_list(n3, "n3_l")
        n4_l = load_list(n4, "n4_l")
        gs_sb = new([P, PACK], F32, "gs_sb")
        nc.sync.dma_start(gs_sb[:], gs.rearrange("(p t) o -> p (t o)", t=PACK))

        xq_w = new([P, S], I32, "xq_w")
        ka_w = new([P, H], I32, "ka_w", "slot_hzb")
        kb_w = new([P, H], I32, "kb_w")
        gather_words(xq_w, x_tab, offs_l)
        gather_words(ka_w, d_tab, ka_l)
        for c in range(2):
            nc.vector.tensor_copy(
                kb_w[:, block(c, S)].bitcast(U32), d_tab[:].bitcast(U32).indirect(kb_l[:, block(c, S // 16)])
            )

        ht_ps = [[ps.tile([P, S], F32, name=f"ht_ps{c}{u}", tag=f"bank{2 * c + u}") for u in range(2)] for c in range(2)]
        ht = [new([P, PACK, P], F32, f"ht{u}") for u in range(2)]
        for c in range(2):
            for u in range(2):
                mx(ht_ps[c][u][:], xq_w[:, block(u)], xa_plane[:, block(u)],
                   ka_w[:, block(c, S)], xa_plane[:, block(c + 1, S)], True, False)
        for c in range(2):
            for u in range(2):
                mx(ht_ps[c][u][:], xq_w[:, block(u)], xa_plane[:, block(u)],
                   kb_w[:, block(c, S)], kb_plane[:, block(c, S)], False, True)
                nc.scalar.activation(
                    ht[u][:, :, block(c, P // 2)], ht_ps[c][u][:].rearrange("p (m t) -> p t m", t=PACK), COPY, scale=0.0625
                )
        h0_ps = [ps.tile([P, P], F32, name=f"h0_ps{u}", tag=f"bank{4 - 4 * u}") for u in range(2)]
        h_ps = [None] + [ps.tile([P, S], F32, name=f"h_ps{t}", tag=f"bank{4 + t}") for t in range(1, PACK)]
        for u in range(2):
            nc.tensor.transpose(h0_ps[u][:], ht[u][:, 0, :], ident[:])
        for t in range(1, PACK):
            for u in range(2):
                nc.tensor.transpose(h_ps[t][:, block(u)], ht[u][:, t, :], ident[:])

        hk_picked = new([P, 2 * H + S], U8, "hk_picked", "slot_hzb")
        gather_bytes(hk_picked[:, 2 * H :], x_bytes, hz_l)
        gather_bytes(hk_picked[:, block(1, H)], d_bytes, k1_l)
        gather_bytes(hk_picked[:, block(0, H)], d_bytes, k2_l)
        place_rows(k12_rows[:], 0, hk_picked[:, block(1, H)], nc.sync)
        place_rows(k12_rows[:], 4, hk_picked[:, block(0, H)], nc.sync)
        place_rows(hz_plane[:], 0, hk_picked[:, 2 * H :], nc.sync)

        h = [new([P, S], F32, f"h{t}") for t in range(PACK)]
        pab = [new([P, 2 * W], F32, f"pab{t}", f"slot{t}") for t in range(PACK)]
        rab = [new([P, 2 * W], F32, f"rab{t}") for t in range(PACK)]
        ub = [new([P, S], F32, f"ub{t}") for t in range(PACK)]
        for t in range(PACK):
            if t == 0:
                for u in range(2):
                    nc.scalar.activation(h[t][:, block(u)], h0_ps[u][:], COPY)
            else:
                nc.vector.tensor_copy(h[t][:], h_ps[t][:])
            nc.scalar.activation(pab[t][:, :W], h[t][:].indirect(n1_l[:]), COPY)
            nc.scalar.activation(pab[t][:, W:], h[t][:].indirect(n2_l[:]), COPY)

        def pair_sums(t):
            nc.vector.tensor_tensor(rab[t][:, :W], pab[t][:, :W], pab[t][:, W:], ALU.add)
            nc.vector.tensor_tensor(rab[t][:, W:], pab[t][:, :W], pab[t][:, W:], ALU.subtract)

        hz_w = new([P, S], I32, "hz_w", "slot0")
        pair_sums(0)
        pair_sums(1)
        gather_words(hz_w, x_tab, hz_l)
        pair_sums(2)
        pair_sums(3)

        for t in range(PACK + 1):
            if t < PACK:
                nc.scalar.activation(ub[t][:].indirect(n1_l[:]), rab[t][:, :W], COPY, scale=0.75)
            if t > 0:
                nc.scalar.activation(ub[t - 1][:].indirect(n2_l[:]), rab[t - 1][:, W:], COPY)

        k2_raw = new([P, H], I32, "k2_raw", "slot3")
        k1_raw = new([P, H], I32, "k1_raw", "slot_z")
        k2_w = new([P, H], I32, "k2_w")
        k1_w = new([P, H], I32, "k1_w")
        k12_plane = new([P, H], U8, "k12_plane")
        z16 = new([P, S, PACK], BF16, "z16", "slot_z")

        def round_z(t, cols):
            nc.vector.tensor_scalar(z16[:, cols, t], ub[t][:, cols], gs_sb[:, t : t + 1], None, ALU.mult)

        gather_words(k2_raw, d_tab, k2_l)
        deal(k12_plane, k12_rows[:])
        deal(k2_w, k2_raw[:])
        gather_words(k1_raw, d_tab, k1_l)
        deal(k1_w, k1_raw[:])
        for t in range(PACK - 1):
            round_z(t, slice(0, S))
        z_w = new([P, S], I32, "z_w")
        z_plane = new([P, S], U8, "z_plane")
        for u in range(2):
            round_z(PACK - 1, block(u))
        for u in range(2):
            nc.vector.quantize_mx(
                out=z_w[:, block(u)].bitcast(FP8X4),
                scales=z_plane[:, block(u)],
                in_=z16[:, block(u), :].rearrange("p c t -> p (c t)"),
            )

        h20_ps = [ps.tile([P, P], F32, name=f"h20_ps{u}", tag=f"bank{4 * u}") for u in range(2)]
        h2_ps = [None] + [ps.tile([P, S], F32, name=f"h2_ps{t}", tag=f"bank{t}") for t in range(1, PACK)]
        for u in range(2):
            mx(h20_ps[u][:], k2_w[:, block(0)], k12_plane[4:P, block(0)],
               hz_w[:, block(u)], hz_plane[:, block(u)], True, False)
        for t in PAGE_ORDER[1:]:
            mx(h2_ps[t][:], k2_w[:, block(t)], k12_plane[4:P, block(t)], hz_w[:], hz_plane[:], True, False)
        for u in range(2):
            mx(h20_ps[u][:], k1_w[:, block(0)], k12_plane[:, block(0)],
               z_w[:, block(u)], z_plane[:, block(u)], False, True)
        for t in PAGE_ORDER[1:]:
            mx(h2_ps[t][:], k1_w[:, block(t)], k12_plane[:, block(t)], z_w[:], z_plane[:], False, True)

        h2 = [new([P, S + SPARE], F32, f"h2_{t}") for t in range(PACK)]
        st = [new([P, S + SPARE], F32, f"st{t}") for t in range(PACK)]
        h2_at = [new([P, S], F32, f"h2_at{t}") for t in range(PACK)]
        st_at = [new([P, S], F32, f"st_at{t}") for t in range(PACK)]
        up = [new([P, S], F32, f"up{t}") for t in range(PACK)]
        page = [new([P, U], F32, f"page{t}") for t in range(PACK)]
        page16 = new([P, U, PACK], BF16, "page16")
        out_rows = out_0.rearrange("(p t) w -> t p w", t=PACK)
        half = U // 2

        def make_st(t):
            if t == 0:
                nc.scalar.activation(h2[t][:, block(0)], h20_ps[0][:], COPY, scale=0.0625)
                nc.vector.tensor_scalar(h2[t][:, block(1)], h20_ps[1][:], 0.0625, None, ALU.mult)
            else:
                nc.vector.tensor_scalar(h2[t][:, :S], h2_ps[t][:], 0.0625, None, ALU.mult)
            nc.scalar.activation(h2_at[t][:], h2[t][:].indirect(n5_l[:]), COPY)
            nc.vector.tensor_tensor(st[t][:, :S], h2[t][:, :S], h2_at[t][:], ALU.subtract)

        def make_up(t):
            nc.scalar.activation(st_at[t][:], st[t][:].indirect(n6_l[:]), COPY)
            nc.vector.tensor_tensor(up[t][:], st[t][:, :S], st_at[t][:], ALU.max)
            nc.scalar.activation(page[t][:].indirect(n3_l[:]), st[t][:, :S], COPY)

        def finish(t):
            nc.scalar.activation(page[t][:].indirect(n4_l[:]), up[t][:], COPY)
            nc.sync.dma_start(out_rows[t], page[t][:])
            if t < PACK - 1:
                nc.vector.tensor_copy(page16[:, :, t], page[t][:])
            else:
                nc.vector.tensor_copy(page16[:, :half, t], page[t][:, :half])
                nc.scalar.activation(page16[:, U - SCALAR_COLS :, t], page[t][:, U - SCALAR_COLS :], COPY)
                nc.vector.tensor_copy(page16[:, half : U - SCALAR_COLS, t], page[t][:, half : U - SCALAR_COLS])

        for step in range(PACK + 2):
            if step < PACK:
                make_st(PAGE_ORDER[step])
            if 1 <= step <= PACK:
                make_up(PAGE_ORDER[step - 1])
            if step >= 2:
                finish(PAGE_ORDER[step - 2])

        out_w = new([P, U], I32, "out_w")
        out_plane = new([P, U], U8, "out_plane")
        words_out = out_1[0].rearrange("p c r -> p (c r)").bitcast(I32)
        for c in range(2):
            cols = slice(c * half, (c + 1) * half)
            nc.vector.quantize_mx(
                out=out_w[:, cols].bitcast(FP8X4),
                scales=out_plane[:, cols],
                in_=page16[:, cols, :].rearrange("p c t -> p (c t)"),
            )
            nc.sync.dma_start(words_out[:, cols], out_w[:, cols])
        for q in range(4):
            queue = nc.scalar if q % 2 else nc.sync
            queue.dma_start(out_2[0].bitcast(I32)[4 * q : 4 * q + 4, :], out_plane[:].bitcast(I32)[32 * q : 32 * q + 4, :])
